import numpy as np
import ml_dtypes


def mxq(x, axis, fmt="e4m3"):
    dtype, down = {"e4m3": (ml_dtypes.float8_e4m3fn, 7), "e5m2": (ml_dtypes.float8_e5m2, 14)}[fmt]
    v = np.moveaxis(np.asarray(x, np.float32).astype(ml_dtypes.bfloat16).astype(np.float64), axis, -1)
    blocks = v.reshape(v.shape[:-1] + (-1, 32))
    amax = np.abs(blocks).max(-1, keepdims=True)
    byte = np.maximum(np.where(amax > 0, np.frexp(amax)[1] - 1 + 127, 0) - down, 1)
    scale = np.exp2(byte - 127.0)
    codes = (blocks / scale).astype(np.float32).astype(dtype).astype(np.float64)
    return np.moveaxis((codes * scale).reshape(v.shape), -1, axis)


WIDE = False


def mx_kscale(k):
    if not WIDE:
        return np.ones(k)
    levels = np.array([10, -10, 5, -5, 0])
    if k % 512:
        return np.exp2(np.random.permutation(np.resize(levels, k // 32))).repeat(32)
    a = np.empty((k // 512, 16))
    for p in range(k // 512):
        a[p, :8] = np.random.permutation(np.resize(levels, 8))
        for g in range(8):
            far = levels[np.abs(levels - a[p, g]) >= 10]
            a[p, g + 8] = far[np.random.randint(len(far))]
    return np.exp2(a.ravel()).repeat(32)


def f64(x):
    return np.asarray(x).astype(np.float64)


def striped(idx):
    return np.tile(idx.reshape(-1, 16).T, (8, 1)).astype(np.uint16)


def unstriped(offs):
    return offs[:16].T.reshape(-1).astype(np.int64)


def striped8(idx):
    return np.concatenate([x.reshape(-1, 16).T for x in idx]).astype(np.uint16)


def runs(offs, k):
    lists = np.stack([offs[16 * r : 16 * r + 16].T.reshape(-1) for r in range(8)]).astype(np.int64)
    return lists[np.arange(k) % 512 // 64]


def pack_weight(w):
    k, n = w.shape
    w = f64(np.asarray(w, np.float32).astype(ml_dtypes.bfloat16)).reshape(k // 32, 32, n)
    amax = np.abs(w).max(1)
    byte = np.clip(np.where(amax > 0, np.frexp(amax)[1] - 1 + 127 - 7, 1), 1, 254)
    scaled = (w * np.exp2(127.0 - byte)[:, None, :]).reshape(k, n).astype(np.float32)
    words = np.ascontiguousarray(scaled.reshape(k // 512, 128, 4, n).transpose(0, 1, 3, 2)).astype(ml_dtypes.float8_e4m3fn).view(np.uint8)
    return words, np.ascontiguousarray(byte.astype(np.uint8).reshape(k // 512, 16, n))


def unpack_weight(words, scales):
    g, p, n, _ = words.shape
    vals = np.ascontiguousarray(words).view(ml_dtypes.float8_e4m3fn).astype(np.float64) * np.repeat(np.exp2(scales.astype(np.float64) - 127.0), 8, axis=1)[..., None]
    return vals.transpose(0, 1, 3, 2).reshape(g * 512, n)


def sigmoid(v):
    return 1.0 / (1.0 + np.exp(-np.maximum(v, -700.0)))

def planes(y):
    n, m = y.shape
    v = y.astype(np.float32).astype(ml_dtypes.bfloat16).astype(np.float64).reshape(n // 32, 32, m)
    top = np.abs(v).max(1)
    byte = np.clip(np.where(top > 0, np.frexp(top)[1] - 1 + 127 - 7, 1), 1, 254)
    codes = (v * np.exp2(127.0 - byte)[:, None, :]).reshape(n, m).astype(np.float32).astype(ml_dtypes.float8_e4m3fn).view(np.uint8)
    words = codes.reshape(n // 512, 128, 4, m).transpose(0, 1, 3, 2)
    return np.ascontiguousarray(words), np.ascontiguousarray(byte.astype(np.uint8).reshape(n // 512, 16, m))


K, T, S, N, H = 512, 2048, 512, 512, 512


def setup_inputs():
    n = np.random.standard_normal
    s = mx_kscale(K)[:, None]
    u = mx_kscale(S)
    packed_xT = pack_weight(n((K, T)) * s)
    packed_w1 = pack_weight(n((S, N)) / np.sqrt(S) / u[:, None])
    return {
        "x_words": packed_xT[0],
        "x_scales": packed_xT[1],
        "wa": (n((K, H)) / np.sqrt(K) / s).astype(np.float32),
        "gt": (np.random.uniform(0.5, 1.5, (S, 1)) * u[:, None]).astype(np.float32),
        "w1_words": packed_w1[0],
        "w1_scales": packed_w1[1],
        "offs": striped(np.random.permutation(T)[:S]),
        "n1": striped8(np.stack([np.random.permutation(H) for _ in range(8)])),
        "n2": striped8(np.stack([np.random.permutation(H) for _ in range(8)])),
        "n3": striped8(np.stack([np.random.permutation(H) for _ in range(8)])),
        "n4": striped8(np.stack([np.random.permutation(H) for _ in range(8)])),
        "n5": striped8(np.stack([np.random.permutation(H) for _ in range(8)])),
    }


def reference(x_words, x_scales, wa, gt, w1_words, w1_scales, offs, n1, n2, n3, n4, n5):
    xq = unpack_weight(x_words, x_scales)[:, unstriped(offs)]
    y = xq.T @ mxq(f64(wa), 0, "e4m3")
    z = f64(gt) * (0.75 * (y[np.arange(S)[:, None], runs(n1, S)] + y[np.arange(S)[:, None], runs(n2, S)]) - y)
    h = unpack_weight(w1_words, w1_scales).T @ mxq(z, 0, "e4m3")
    out_0 = (h[np.arange(N)[:, None], runs(n3, N)]) * sigmoid(h) + (h[np.arange(N)[:, None], runs(n4, N)]) * (sigmoid(h[np.arange(N)[:, None], runs(n5, N)]))
    return (out_0,) + planes(out_0)

@@ -1,0 +1,228 @@
+from contextlib import ExitStack
+
+import concourse.mybir as mybir
+
+F32 = mybir.dt.float32
+BF16 = mybir.dt.bfloat16
+I32 = mybir.dt.int32
+U32 = mybir.dt.uint32
+U16 = mybir.dt.uint16
+U8 = mybir.dt.uint8
+FP8X4 = mybir.dt.float8_e4m3fn_x4
+ADD = mybir.AluOpType.add
+MULT = mybir.AluOpType.mult
+COPY = mybir.ActivationFunctionType.Copy
+SIGMOID = mybir.ActivationFunctionType.Sigmoid
+
+FLOPS = 2 * 512 * 512 * 512 * 2
+
+P = 128
+PACK = 4
+T = 2048
+S = 512
+H = 512
+BANK = 512
+PER_COL = 16
+
+WA_LOADS = [(0, 384), (384, 512)]
+WA_PASSES = [(0, 256), (256, 384), (384, 512)]
+Z_CHUNKS = [(0, 256), (256, 384), (384, 512)]
+OUT_CHUNKS = [(0, 128), (128, 256), (256, 384), (384, 512)]
+
+
+def tile_picked_toklapwsum_none_po_kernel(
+    tc, x_words, x_scales, wa, gt, w1_words, w1_scales, offs, n1, n2, n3, n4, n5, out_0, out_1, out_2
+):
+    nc = tc.nc
+    with ExitStack() as ctx:
+        keep = ctx.enter_context(tc.tile_pool(name="keep", bufs=1))
+        psum = ctx.enter_context(tc.psum_pool(name="psum", bufs=1))
+
+        def sb(name, shape, dtype):
+            return keep.tile(shape, dtype, name=name, align_bytes=64)
+
+        def load_list(name, dram):
+            tile = sb(name, [P, S // PER_COL], U16)
+            nc.sync.dma_start(tile[:], dram)
+            return tile
+
+        def load_scale_rows(queue, tile, dram):
+            for q in range(4):
+                queue.dma_start(tile[32 * q : 32 * q + 4, :].bitcast(I32), dram[0, 4 * q : 4 * q + 4, :].bitcast(I32))
+
+        def entries(tile, lo, hi):
+            return tile[:, lo // PER_COL : hi // PER_COL]
+
+        def deal(dst, src, run):
+            nc.vector.tensor_copy(
+                dst.rearrange("k t (c i) -> k c t i", i=run),
+                src.rearrange("k (c i t) -> k c t i", i=run, t=PACK),
+            )
+
+        def rows_by_four(planes):
+            return planes.rearrange("p t (c i) -> p c t i", i=4)
+
+        def words_by_four(grouped):
+            return grouped.rearrange("p (c i) t -> p c t i", i=4)
+
+        def banks_for(name, lo, hi):
+            width = hi - lo
+            per_bank = BANK // width
+            banks = [psum.tile([P, per_bank, width], F32, name="%s_%d_%d" % (name, lo, b)) for b in range(PACK // per_bank)]
+            return [banks[t // per_bank][:, t % per_bank, :] for t in range(PACK)]
+
+        x_plane = sb("x_plane", [P, T], U8)
+        nc.vector.memset(x_plane[:].bitcast(I32), 0)
+        w1_plane = sb("w1_plane", [P, S], U8)
+        nc.vector.memset(w1_plane[:].bitcast(I32), 0)
+
+        wa_rows = wa.rearrange("(p t) j -> p t j", t=PACK)
+        wa_raw = [sb("wa_raw%d" % lo, [P, PACK, hi - lo], F32) for lo, hi in WA_LOADS]
+        offs_t = load_list("offs_t", offs)
+        nc.sync.dma_start(wa_raw[0][:], wa_rows[:, :, slice(*WA_LOADS[0])])
+        load_scale_rows(nc.sync, x_plane, x_scales)
+        x_table = sb("x_table", [P, T], U32)
+        nc.sync.dma_start(x_table[:].bitcast(I32), x_words[0].rearrange("p n t -> p (n t)").bitcast(I32))
+        nc.sync.dma_start(wa_raw[1][:], wa_rows[:, :, slice(*WA_LOADS[1])])
+        gt_t = sb("gt_t", [P, PACK], F32)
+        nc.sync.dma_start(gt_t[:], gt.rearrange("(p t) o -> p (t o)", t=PACK))
+        n2_t = load_list("n2_t", n2)
+        n1_t = load_list("n1_t", n1)
+        w1_table = sb("w1_table", [P, S], I32)
+        nc.sync.dma_start(w1_table[:], w1_words[0].rearrange("p n t -> p (n t)").bitcast(I32))
+        load_scale_rows(nc.sync, w1_plane, w1_scales)
+        n5_t = load_list("n5_t", n5)
+        n3_t = load_list("n3_t", n3)
+        n4_t = load_list("n4_t", n4)
+
+        wa_codes = sb("wa_codes", [P, H], U32)
+        wa_plane = sb("wa_plane", [P, H], U8)
+
+        def quantise_wa(n):
+            lo, hi = WA_LOADS[n]
+            grouped = sb("wa_grouped%d" % lo, [P, hi - lo, PACK], BF16)
+            nc.scalar.copy(words_by_four(grouped[:]), rows_by_four(wa_raw[n][:]))
+            nc.vector.quantize_mx(wa_codes[:, lo:hi].bitcast(FP8X4), wa_plane[:, lo:hi], grouped[:].rearrange("p c t -> p (c t)"))
+
+        x_bytes = sb("x_bytes", [P, S], U8)
+        nc.vector.tensor_copy(x_bytes[:], x_plane[:].indirect(offs_t[:]))
+        x_dealt_bytes = sb("x_dealt_bytes", [P, PACK, P], U8)
+        deal(x_dealt_bytes[:], x_bytes[:], 16)
+        quantise_wa(0)
+        x_codes = sb("x_codes", [P, PACK, P], U32)
+        nc.vector.tensor_copy(x_codes[:].rearrange("k t m -> k m t"), x_table[:].indirect(offs_t[:]))
+        quantise_wa(1)
+        gt_mix = sb("gt_mix", [P, PACK], F32)
+        nc.vector.tensor_scalar(gt_mix[:], gt_t[:], 0.75, None, MULT)
+
+        y_win = [sb("y_win%d" % t, [P, H], F32) for t in range(PACK)]
+        for t in range(PACK):
+            acc = psum.tile([P, H], F32, name="y_acc%d" % t)
+            for lo, hi in WA_PASSES:
+                nc.tensor.matmul_mx(
+                    acc[:, lo:hi], x_codes[:, t, :].bitcast(FP8X4), x_dealt_bytes[:, t, :],
+                    wa_codes[:, lo:hi].bitcast(FP8X4), wa_plane[:, lo:hi], start=True, stop=True,
+                )
+            nc.scalar.activation(y_win[t][:], acc[:], COPY, scale=gt_mix[:, t : t + 1])
+
+        w1_codes = sb("w1_codes", [P, PACK, P], I32)
+        deal(w1_codes[:], w1_table[:], 4)
+        w1_dealt_bytes = sb("w1_dealt_bytes", [P, PACK, P], U8)
+        deal(w1_dealt_bytes[:], w1_plane[:], 16)
+
+        z_codes = sb("z_codes", [P, H], U32)
+        z_plane = sb("z_plane", [P, H], U8)
+        h_win = [sb("h_win%d" % t, [P, H], F32) for t in range(PACK)]
+        h_gate = sb("h_gate", [P, PACK, H], F32)
+        own = [sb("own%d" % t, [P, H], F32) for t in range(PACK)]
+        first = [sb("first%d" % lo, [P, PACK, hi - lo], F32) for lo, hi in Z_CHUNKS]
+        second = [sb("second%d" % lo, [P, PACK, hi - lo], F32) for lo, hi in Z_CHUNKS]
+        h_acc = [banks_for("h", lo, hi) for lo, hi in Z_CHUNKS]
+
+        def look_up_y(n):
+            lo, hi = Z_CHUNKS[n]
+            for t in range(PACK):
+                if n == 0:
+                    nc.vector.tensor_scalar(own[t][:], y_win[t][:], -4.0 / 3.0, None, MULT)
+                nc.scalar.activation(first[n][:, t, :], y_win[t][:].indirect(entries(n1_t, lo, hi)), COPY)
+                nc.vector.tensor_tensor(second[n][:, t, :], y_win[t][:].indirect(entries(n2_t, lo, hi)), own[t][:, lo:hi], ADD)
+
+        def multiply_z(n):
+            lo, hi = Z_CHUNKS[n]
+            grouped = sb("z_grouped%d" % lo, [P, hi - lo, PACK], BF16)
+            nc.vector.tensor_tensor(words_by_four(grouped[:]), rows_by_four(first[n][:]), rows_by_four(second[n][:]), ADD)
+            nc.vector.quantize_mx(z_codes[:, lo:hi].bitcast(FP8X4), z_plane[:, lo:hi], grouped[:].rearrange("p c t -> p (c t)"))
+            for t in range(PACK):
+                nc.tensor.matmul_mx(
+                    h_acc[n][t], w1_codes[:, t, :].bitcast(FP8X4), w1_dealt_bytes[:, t, :],
+                    z_codes[:, lo:hi].bitcast(FP8X4), z_plane[:, lo:hi], start=True, stop=True,
+                )
+
+        def fetch_h(n):
+            lo, hi = Z_CHUNKS[n]
+            for t in range(PACK):
+                nc.scalar.copy(h_win[t][:, lo:hi], h_acc[n][t])
+
+        def gate_h(n):
+            lo, hi = Z_CHUNKS[n]
+            for t in range(PACK):
+                nc.scalar.activation(h_gate[:, t, lo:hi], h_acc[n][t], SIGMOID)
+
+        look_up_y(0)
+        look_up_y(1)
+        multiply_z(0)
+        look_up_y(2)
+        fetch_h(0)
+        multiply_z(1)
+        gate_h(0)
+        fetch_h(1)
+        multiply_z(2)
+        gate_h(1)
+        fetch_h(2)
+
+        out_rows = out_0.rearrange("(p t) j -> p t j", t=PACK)
+        out_words = out_1[0].rearrange("p n t -> p (n t)").bitcast(I32)
+        out_plane = sb("out_plane", [P, H], U8)
+        result = [sb("result%d" % lo, [P, PACK, hi - lo], F32) for lo, hi in OUT_CHUNKS]
+        out_grouped = [sb("out_grouped%d" % lo, [P, hi - lo, PACK], BF16) for lo, hi in OUT_CHUNKS]
+
+        def look_up_h(n):
+            lo, hi = OUT_CHUNKS[n]
+            third = sb("third%d" % lo, [P, PACK, hi - lo], F32)
+            fifth = sb("fifth%d" % lo, [P, PACK, hi - lo], F32)
+            left = sb("left%d" % lo, [P, PACK, hi - lo], F32)
+            right = sb("right%d" % lo, [P, PACK, hi - lo], F32)
+            for t in range(PACK):
+                nc.scalar.activation(fifth[:, t, :], h_win[t][:].indirect(entries(n5_t, lo, hi)), SIGMOID)
+                nc.vector.tensor_tensor(right[:, t, :], h_win[t][:].indirect(entries(n4_t, lo, hi)), fifth[:, t, :], MULT)
+            for t in range(PACK):
+                nc.scalar.activation(third[:, t, :], h_win[t][:].indirect(entries(n3_t, lo, hi)), COPY)
+            nc.vector.tensor_tensor(left[:], third[:], h_gate[:, :, lo:hi], MULT)
+            nc.vector.tensor_tensor(result[n][:], left[:], right[:], ADD)
+            nc.sync.dma_start(out_rows[:, :, lo:hi], result[n][:])
+
+        def round_out(n, copy):
+            copy(words_by_four(out_grouped[n][:]), rows_by_four(result[n][:]))
+
+        def quantise_out(n):
+            lo, hi = OUT_CHUNKS[n]
+            codes = sb("out_codes%d" % lo, [P, hi - lo], U32)
+            nc.vector.quantize_mx(codes[:].bitcast(FP8X4), out_plane[:, lo:hi], out_grouped[n][:].rearrange("p c t -> p (c t)"))
+            nc.sync.dma_start(out_words[:, lo:hi], codes[:].bitcast(I32))
+
+        look_up_h(0)
+        round_out(0, nc.vector.tensor_copy)
+        look_up_h(1)
+        quantise_out(0)
+        round_out(1, nc.vector.tensor_copy)
+        gate_h(2)
+        look_up_h(2)
+        quantise_out(1)
+        look_up_h(3)
+        round_out(2, nc.scalar.copy)
+        round_out(3, nc.vector.tensor_copy)
+        quantise_out(2)
+        quantise_out(3)
+        for q in range(4):
+            queue = nc.sync if q % 2 == 0 else nc.scalar
+            queue.dma_start(out_2[0, 4 * q : 4 * q + 4, :].bitcast(I32), out_plane[32 * q : 32 * q + 4, :].bitcast(I32))

@@ -24,10 +24,10 @@ H = 512
 BANK = 512
 PER_COL = 16
 
-WA_LOADS = [(0, 384), (384, 512)]
-WA_PASSES = [(0, 256), (256, 384), (384, 512)]
-Z_CHUNKS = [(0, 256), (256, 384), (384, 512)]
-OUT_CHUNKS = [(0, 128), (128, 256), (256, 384), (384, 512)]
+HALVES = [(0, 256), (256, 512)]
+LAST_PIECES = [(0, 256), (256, 384), (384, 512)]
+WINDOW = 1024
+WA_SCALAR_COLS = 96
 
 
 def tile_picked_toklapwsum_none_po_kernel(
@@ -38,8 +38,8 @@ def tile_picked_toklapwsum_none_po_kernel(
         keep = ctx.enter_context(tc.tile_pool(name="keep", bufs=1))
         psum = ctx.enter_context(tc.psum_pool(name="psum", bufs=1))
 
-        def sb(name, shape, dtype):
-            return keep.tile(shape, dtype, name=name, align_bytes=64)
+        def sb(name, shape, dtype, tag=None):
+            return keep.tile(shape, dtype, name=name, tag=tag or name, align_bytes=64)
 
         def load_list(name, dram):
             tile = sb(name, [P, S // PER_COL], U16)
@@ -77,152 +77,197 @@ def tile_picked_toklapwsum_none_po_kernel(
         nc.vector.memset(w1_plane[:].bitcast(I32), 0)
 
         wa_rows = wa.rearrange("(p t) j -> p t j", t=PACK)
-        wa_raw = [sb("wa_raw%d" % lo, [P, PACK, hi - lo], F32) for lo, hi in WA_LOADS]
+        wa_raw = [sb("wa_raw%d" % lo, [P, PACK, hi - lo], F32) for lo, hi in HALVES]
         offs_t = load_list("offs_t", offs)
-        nc.sync.dma_start(wa_raw[0][:], wa_rows[:, :, slice(*WA_LOADS[0])])
+        nc.sync.dma_start(wa_raw[0][:], wa_rows[:, :, slice(*HALVES[0])])
         load_scale_rows(nc.sync, x_plane, x_scales)
         x_table = sb("x_table", [P, T], U32)
         nc.sync.dma_start(x_table[:].bitcast(I32), x_words[0].rearrange("p n t -> p (n t)").bitcast(I32))
-        nc.sync.dma_start(wa_raw[1][:], wa_rows[:, :, slice(*WA_LOADS[1])])
+        nc.sync.dma_start(wa_raw[1][:], wa_rows[:, :, slice(*HALVES[1])])
         gt_t = sb("gt_t", [P, PACK], F32)
         nc.sync.dma_start(gt_t[:], gt.rearrange("(p t) o -> p (t o)", t=PACK))
-        n2_t = load_list("n2_t", n2)
-        n1_t = load_list("n1_t", n1)
+        load_scale_rows(nc.sync, w1_plane, w1_scales)
         w1_table = sb("w1_table", [P, S], I32)
         nc.sync.dma_start(w1_table[:], w1_words[0].rearrange("p n t -> p (n t)").bitcast(I32))
-        load_scale_rows(nc.sync, w1_plane, w1_scales)
+        n2_t = load_list("n2_t", n2)
+        n1_t = load_list("n1_t", n1)
         n5_t = load_list("n5_t", n5)
-        n3_t = load_list("n3_t", n3)
         n4_t = load_list("n4_t", n4)
+        n3_t = load_list("n3_t", n3)
 
         wa_codes = sb("wa_codes", [P, H], U32)
         wa_plane = sb("wa_plane", [P, H], U8)
 
-        def quantise_wa(n):
-            lo, hi = WA_LOADS[n]
-            grouped = sb("wa_grouped%d" % lo, [P, hi - lo, PACK], BF16)
-            nc.scalar.copy(words_by_four(grouped[:]), rows_by_four(wa_raw[n][:]))
+        def quantise_wa(n, cut):
+            lo, hi = HALVES[n]
+            grouped = sb("wa_grouped%d" % lo, [P, hi - lo, PACK], BF16, "staging%d" % n)
+            nc.scalar.copy(words_by_four(grouped[:, :cut, :]), rows_by_four(wa_raw[n][:, :, :cut]))
+            if cut < hi - lo:
+                nc.vector.tensor_copy(words_by_four(grouped[:, cut:, :]), rows_by_four(wa_raw[n][:, :, cut:]))
             nc.vector.quantize_mx(wa_codes[:, lo:hi].bitcast(FP8X4), wa_plane[:, lo:hi], grouped[:].rearrange("p c t -> p (c t)"))
 
         x_bytes = sb("x_bytes", [P, S], U8)
         nc.vector.tensor_copy(x_bytes[:], x_plane[:].indirect(offs_t[:]))
         x_dealt_bytes = sb("x_dealt_bytes", [P, PACK, P], U8)
         deal(x_dealt_bytes[:], x_bytes[:], 16)
-        quantise_wa(0)
+        quantise_wa(0, 256)
         x_codes = sb("x_codes", [P, PACK, P], U32)
         nc.vector.tensor_copy(x_codes[:].rearrange("k t m -> k m t"), x_table[:].indirect(offs_t[:]))
-        quantise_wa(1)
+        quantise_wa(1, WA_SCALAR_COLS)
         gt_mix = sb("gt_mix", [P, PACK], F32)
         nc.vector.tensor_scalar(gt_mix[:], gt_t[:], 0.75, None, MULT)
+        gt_neg = sb("gt_neg", [P, PACK], F32)
+        nc.vector.tensor_scalar(gt_neg[:], gt_t[:], -1.0, None, MULT)
 
         y_win = [sb("y_win%d" % t, [P, H], F32) for t in range(PACK)]
-        for t in range(PACK):
-            acc = psum.tile([P, H], F32, name="y_acc%d" % t)
-            for lo, hi in WA_PASSES:
-                nc.tensor.matmul_mx(
-                    acc[:, lo:hi], x_codes[:, t, :].bitcast(FP8X4), x_dealt_bytes[:, t, :],
-                    wa_codes[:, lo:hi].bitcast(FP8X4), wa_plane[:, lo:hi], start=True, stop=True,
-                )
-            nc.scalar.activation(y_win[t][:], acc[:], COPY, scale=gt_mix[:, t : t + 1])
+        own = [sb("own%d" % t, [P, H], F32) for t in range(PACK)]
 
-        w1_codes = sb("w1_codes", [P, PACK, P], I32)
+        def product(name, n, t, codes, planes, moving, moving_plane):
+            lo, hi = HALVES[n]
+            acc = psum.tile([P, hi - lo], F32, name="%s%d_%d" % (name, n, t), tag="bank%d" % (PACK * n + t))
+            nc.tensor.matmul_mx(
+                acc[:], codes[:, t, :].bitcast(FP8X4), planes[:, t, :],
+                moving[:, lo:hi].bitcast(FP8X4), moving_plane[:, lo:hi], start=True, stop=True,
+            )
+            return acc
+
+        def own_term(n, t):
+            lo, hi = HALVES[n]
+            nc.vector.tensor_scalar(own[t][:, lo:hi], y_win[t][:, lo:hi], -4.0 / 3.0, None, MULT)
+
+        def own_from_bank(n, t):
+            lo, hi = HALVES[n]
+            nc.scalar.activation(own[t][:, lo:hi], y_acc[n, t][:], COPY, scale=gt_neg[:, t : t + 1])
+
+        y_acc = {}
+        for n, (lo, hi) in enumerate(HALVES):
+            for t in range(PACK):
+                y_acc[n, t] = product("y_acc", n, t, x_codes, x_dealt_bytes, wa_codes, wa_plane)
+                nc.scalar.activation(y_win[t][:, lo:hi], y_acc[n, t][:], COPY, scale=gt_mix[:, t : t + 1])
+
+        w1_codes = sb("w1_codes", [P, PACK, P], I32, "staging1")
         deal(w1_codes[:], w1_table[:], 4)
         w1_dealt_bytes = sb("w1_dealt_bytes", [P, PACK, P], U8)
         deal(w1_dealt_bytes[:], w1_plane[:], 16)
+        for t in range(PACK):
+            own_term(0, t)
 
         z_codes = sb("z_codes", [P, H], U32)
         z_plane = sb("z_plane", [P, H], U8)
         h_win = [sb("h_win%d" % t, [P, H], F32) for t in range(PACK)]
-        h_gate = sb("h_gate", [P, PACK, H], F32)
-        own = [sb("own%d" % t, [P, H], F32) for t in range(PACK)]
-        first = [sb("first%d" % lo, [P, PACK, hi - lo], F32) for lo, hi in Z_CHUNKS]
-        second = [sb("second%d" % lo, [P, PACK, hi - lo], F32) for lo, hi in Z_CHUNKS]
-        h_acc = [banks_for("h", lo, hi) for lo, hi in Z_CHUNKS]
+        h_gate = [sb("h_gate%d" % t, [P, H], F32) for t in range(PACK)]
+        first = sb("first", [P, PACK, H], F32)
+        second = sb("second", [P, PACK, H], F32)
+        z_grouped = sb("z_grouped", [P, H, PACK], BF16)
+        h_acc = {}
 
-        def look_up_y(n):
-            lo, hi = Z_CHUNKS[n]
-            for t in range(PACK):
-                if n == 0:
-                    nc.vector.tensor_scalar(own[t][:], y_win[t][:], -4.0 / 3.0, None, MULT)
-                nc.scalar.activation(first[n][:, t, :], y_win[t][:].indirect(entries(n1_t, lo, hi)), COPY)
-                nc.vector.tensor_tensor(second[n][:, t, :], y_win[t][:].indirect(entries(n2_t, lo, hi)), own[t][:, lo:hi], ADD)
+        def first_term(t, lo, hi):
+            nc.scalar.activation(first[:, t, lo:hi], y_win[t][:].indirect(entries(n1_t, lo, hi)), COPY)
+
+        def second_term(t, lo, hi):
+            nc.vector.tensor_tensor(second[:, t, lo:hi], y_win[t][:].indirect(entries(n2_t, lo, hi)), own[t][:, lo:hi], ADD)
+
+        def sum_z(lo, hi):
+            nc.vector.tensor_tensor(words_by_four(z_grouped[:, lo:hi, :]), rows_by_four(first[:, :, lo:hi]), rows_by_four(second[:, :, lo:hi]), ADD)
 
         def multiply_z(n):
-            lo, hi = Z_CHUNKS[n]
-            grouped = sb("z_grouped%d" % lo, [P, hi - lo, PACK], BF16)
-            nc.vector.tensor_tensor(words_by_four(grouped[:]), rows_by_four(first[n][:]), rows_by_four(second[n][:]), ADD)
-            nc.vector.quantize_mx(z_codes[:, lo:hi].bitcast(FP8X4), z_plane[:, lo:hi], grouped[:].rearrange("p c t -> p (c t)"))
+            lo, hi = HALVES[n]
+            nc.vector.quantize_mx(z_codes[:, lo:hi].bitcast(FP8X4), z_plane[:, lo:hi], z_grouped[:, lo:hi, :].rearrange("p c t -> p (c t)"))
             for t in range(PACK):
-                nc.tensor.matmul_mx(
-                    h_acc[n][t], w1_codes[:, t, :].bitcast(FP8X4), w1_dealt_bytes[:, t, :],
-                    z_codes[:, lo:hi].bitcast(FP8X4), z_plane[:, lo:hi], start=True, stop=True,
-                )
+                h_acc[n, t] = product("h_acc", n, t, w1_codes, w1_dealt_bytes, z_codes, z_plane)
 
-        def fetch_h(n):
-            lo, hi = Z_CHUNKS[n]
-            for t in range(PACK):
-                nc.scalar.copy(h_win[t][:, lo:hi], h_acc[n][t])
+        def fetch_h(n, t, copy):
+            lo, hi = HALVES[n]
+            copy(h_win[t][:, lo:hi], h_acc[n, t][:])
 
-        def gate_h(n):
-            lo, hi = Z_CHUNKS[n]
-            for t in range(PACK):
-                nc.scalar.activation(h_gate[:, t, lo:hi], h_acc[n][t], SIGMOID)
+        def gate_h(n, t):
+            lo, hi = HALVES[n]
+            nc.scalar.activation(h_gate[t][:, lo:hi], h_acc[n, t][:], SIGMOID)
 
-        look_up_y(0)
-        look_up_y(1)
-        multiply_z(0)
-        look_up_y(2)
-        fetch_h(0)
+        for t in range(PACK):
+            first_term(t, 0, 256)
+            second_term(t, 0, 256)
+        sum_z(0, 256)
+        for t in range(PACK):
+            if t < 2:
+                own_term(1, t)
+            else:
+                own_from_bank(1, t)
+        for t in range(PACK):
+            first_term(t, 256, H)
+            second_term(t, 256, H)
+            if t == 0:
+                multiply_z(0)
+        for t in range(PACK):
+            fetch_h(0, t, nc.scalar.copy)
+        sum_z(256, H)
         multiply_z(1)
-        gate_h(0)
-        fetch_h(1)
-        multiply_z(2)
-        gate_h(1)
-        fetch_h(2)
+        for t in range(PACK):
+            gate_h(0, t)
+        for t in range(PACK):
+            fetch_h(1, t, nc.vector.tensor_copy)
 
         out_rows = out_0.rearrange("(p t) j -> p t j", t=PACK)
         out_words = out_1[0].rearrange("p n t -> p (n t)").bitcast(I32)
         out_plane = sb("out_plane", [P, H], U8)
-        result = [sb("result%d" % lo, [P, PACK, hi - lo], F32) for lo, hi in OUT_CHUNKS]
-        out_grouped = [sb("out_grouped%d" % lo, [P, hi - lo, PACK], BF16) for lo, hi in OUT_CHUNKS]
+        out_codes = sb("out_codes", [P, H], U32)
+        result = sb("result", [P, PACK, H], F32)
+        out_grouped = sb("out_grouped", [P, H, PACK], BF16)
+        third = [sb("third%d" % t, [P, H], F32) for t in range(PACK)]
+        fifth = [sb("fifth%d" % t, [P, H], F32) for t in range(PACK)]
+        left = [sb("left%d" % t, [P, H], F32) for t in range(PACK)]
+        right = [sb("right%d" % t, [P, H], F32) for t in range(PACK)]
 
-        def look_up_h(n):
-            lo, hi = OUT_CHUNKS[n]
-            third = sb("third%d" % lo, [P, PACK, hi - lo], F32)
-            fifth = sb("fifth%d" % lo, [P, PACK, hi - lo], F32)
-            left = sb("left%d" % lo, [P, PACK, hi - lo], F32)
-            right = sb("right%d" % lo, [P, PACK, hi - lo], F32)
-            for t in range(PACK):
-                nc.scalar.activation(fifth[:, t, :], h_win[t][:].indirect(entries(n5_t, lo, hi)), SIGMOID)
-                nc.vector.tensor_tensor(right[:, t, :], h_win[t][:].indirect(entries(n4_t, lo, hi)), fifth[:, t, :], MULT)
-            for t in range(PACK):
-                nc.scalar.activation(third[:, t, :], h_win[t][:].indirect(entries(n3_t, lo, hi)), COPY)
-            nc.vector.tensor_tensor(left[:], third[:], h_gate[:, :, lo:hi], MULT)
-            nc.vector.tensor_tensor(result[n][:], left[:], right[:], ADD)
-            nc.sync.dma_start(out_rows[:, :, lo:hi], result[n][:])
+        def g5(t, lo, hi):
+            nc.scalar.activation(fifth[t][:, lo:hi], h_win[t][:].indirect(entries(n5_t, lo, hi)), SIGMOID)
 
-        def round_out(n, copy):
-            copy(words_by_four(out_grouped[n][:]), rows_by_four(result[n][:]))
+        def p4(t, lo, hi):
+            nc.vector.tensor_tensor(right[t][:, lo:hi], h_win[t][:].indirect(entries(n4_t, lo, hi)), fifth[t][:, lo:hi], MULT)
 
-        def quantise_out(n):
-            lo, hi = OUT_CHUNKS[n]
-            codes = sb("out_codes%d" % lo, [P, hi - lo], U32)
-            nc.vector.quantize_mx(codes[:].bitcast(FP8X4), out_plane[:, lo:hi], out_grouped[n][:].rearrange("p c t -> p (c t)"))
-            nc.sync.dma_start(out_words[:, lo:hi], codes[:].bitcast(I32))
+        def g3(t, lo, hi):
+            nc.scalar.activation(third[t][:, lo:hi], h_win[t][:].indirect(entries(n3_t, lo, hi)), COPY)
 
-        look_up_h(0)
-        round_out(0, nc.vector.tensor_copy)
-        look_up_h(1)
-        quantise_out(0)
-        round_out(1, nc.vector.tensor_copy)
-        gate_h(2)
-        look_up_h(2)
-        quantise_out(1)
-        look_up_h(3)
-        round_out(2, nc.scalar.copy)
-        round_out(3, nc.vector.tensor_copy)
-        quantise_out(2)
-        quantise_out(3)
+        def p3(t, lo, hi):
+            nc.vector.tensor_tensor(left[t][:, lo:hi], third[t][:, lo:hi], h_gate[t][:, lo:hi], MULT)
+
+        def add(t, lo, hi):
+            nc.vector.tensor_tensor(result[:, t, lo:hi], left[t][:, lo:hi], right[t][:, lo:hi], ADD)
+
+        def store(t0, t1, lo, hi):
+            nc.sync.dma_start(out_rows[:, t0:t1, lo:hi], result[:, t0:t1, lo:hi])
+
+        def rnd(t0, t1, lo, hi, copy=nc.vector.tensor_copy):
+            copy(words_by_four(out_grouped[:, lo:hi, t0:t1]), rows_by_four(result[:, t0:t1, lo:hi]))
+
+        def quant(lo, hi):
+            nc.vector.quantize_mx(out_codes[:, lo:hi].bitcast(FP8X4), out_plane[:, lo:hi], out_grouped[:, lo:hi, :].rearrange("p c t -> p (c t)"))
+
+        def store_words(lo, hi):
+            nc.sync.dma_start(out_words[:, lo:hi], out_codes[:, lo:hi].bitcast(I32))
+
+        for t in range(4):
+            g5(t, 0, 256); p4(t, 0, 256)
+            if t > 0:
+                add(t - 1, 0, 256)
+            g3(t, 0, 256); p3(t, 0, 256)
+        for t in range(4):
+            g5(t, 256, H); p4(t, 256, H)
+            if t == 0:
+                add(3, 0, 256); store(0, 4, 0, 256)
+            else:
+                add(t - 1, 256, H)
+            gate_h(1, t)
+            if t < 3:
+                g3(t, 256, H); p3(t, 256, H)
+            if t == 0:
+                rnd(0, 4, 0, 256)
+            if t == 1:
+                quant(0, 256); store_words(0, 256)
+            if t == 2:
+                store(0, 2, 256, H); rnd(0, 2, 256, H)
+        g3(3, 256, 384); p3(3, 256, 384)
+        g3(3, 384, H); p3(3, 384, H); add(3, 256, 384); add(3, 384, H); store(2, 4, 256, H); rnd(2, 4, 256, 384); rnd(2, 4, 384, H); quant(256, 384); quant(384, H); store_words(256, H)
+
         for q in range(4):
             queue = nc.sync if q % 2 == 0 else nc.scalar
             queue.dma_start(out_2[0, 4 * q : 4 * q + 4, :].bitcast(I32), out_plane[32 * q : 32 * q + 4, :].bitcast(I32))

@@ -71,6 +71,9 @@ def tile_picked_toklapwsum_none_po_kernel(
             banks = [psum.tile([P, per_bank, width], F32, name="%s_%d_%d" % (name, lo, b)) for b in range(PACK // per_bank)]
             return [banks[t // per_bank][:, t % per_bank, :] for t in range(PACK)]
 
+        warm = sb("warm", [P, 8], F32)
+        nc.gpsimd.memset(warm[:, 0:1], 0.0)
+        nc.scalar.activation(warm[:, 4:5], warm[:, 0:1], SIGMOID)
         x_plane = sb("x_plane", [P, T], U8)
         nc.vector.memset(x_plane[:].bitcast(I32), 0)
         w1_plane = sb("w1_plane", [P, S], U8)
@@ -156,23 +159,28 @@ def tile_picked_toklapwsum_none_po_kernel(
         z_plane = sb("z_plane", [P, H], U8)
         h_win = [sb("h_win%d" % t, [P, H], F32) for t in range(PACK)]
         h_gate = [sb("h_gate%d" % t, [P, H], F32) for t in range(PACK)]
-        first = sb("first", [P, PACK, H], F32)
-        second = sb("second", [P, PACK, H], F32)
-        z_grouped = sb("z_grouped", [P, H, PACK], BF16)
+        first = [sb("first%d" % lo, [P, PACK, hi - lo], F32) for lo, hi in HALVES]
+        second = {}
+        z_grouped = {}
         h_acc = {}
 
-        def first_term(t, lo, hi):
-            nc.scalar.activation(first[:, t, lo:hi], y_win[t][:].indirect(entries(n1_t, lo, hi)), COPY)
+        def first_term(n, t):
+            lo, hi = HALVES[n]
+            nc.scalar.activation(first[n][:, t, :], y_win[t][:].indirect(entries(n1_t, lo, hi)), COPY)
 
-        def second_term(t, lo, hi):
-            nc.vector.tensor_tensor(second[:, t, lo:hi], y_win[t][:].indirect(entries(n2_t, lo, hi)), own[t][:, lo:hi], ADD)
+        def second_term(n, t):
+            lo, hi = HALVES[n]
+            if t == 0:
+                second[n] = sb("second%d" % lo, [P, PACK, hi - lo], F32, None)
+            nc.vector.tensor_tensor(second[n][:, t, :], y_win[t][:].indirect(entries(n2_t, lo, hi)), own[t][:, lo:hi], ADD)
 
-        def sum_z(lo, hi):
-            nc.vector.tensor_tensor(words_by_four(z_grouped[:, lo:hi, :]), rows_by_four(first[:, :, lo:hi]), rows_by_four(second[:, :, lo:hi]), ADD)
+        def sum_z(n):
+            z_grouped[n] = sb("z_grouped%d" % n, [P, H // 2, PACK], BF16, "z_grouped")
+            nc.vector.tensor_tensor(words_by_four(z_grouped[n][:]), rows_by_four(first[n][:]), rows_by_four(second[n][:]), ADD)
 
         def multiply_z(n):
             lo, hi = HALVES[n]
-            nc.vector.quantize_mx(z_codes[:, lo:hi].bitcast(FP8X4), z_plane[:, lo:hi], z_grouped[:, lo:hi, :].rearrange("p c t -> p (c t)"))
+            nc.vector.quantize_mx(z_codes[:, lo:hi].bitcast(FP8X4), z_plane[:, lo:hi], z_grouped[n][:].rearrange("p c t -> p (c t)"))
             for t in range(PACK):
                 h_acc[n, t] = product("h_acc", n, t, w1_codes, w1_dealt_bytes, z_codes, z_plane)
 
@@ -185,22 +193,22 @@ def tile_picked_toklapwsum_none_po_kernel(
             nc.scalar.activation(h_gate[t][:, lo:hi], h_acc[n, t][:], SIGMOID)
 
         for t in range(PACK):
-            first_term(t, 0, 256)
-            second_term(t, 0, 256)
-        sum_z(0, 256)
+            first_term(0, t)
+            second_term(0, t)
         for t in range(PACK):
             if t < 2:
                 own_term(1, t)
             else:
                 own_from_bank(1, t)
+        sum_z(0)
         for t in range(PACK):
-            first_term(t, 256, H)
-            second_term(t, 256, H)
+            first_term(1, t)
+            second_term(1, t)
             if t == 0:
                 multiply_z(0)
         for t in range(PACK):
             fetch_h(0, t, nc.scalar.copy)
-        sum_z(256, H)
+        sum_z(1)
         multiply_z(1)
         for t in range(PACK):
             gate_h(0, t)
@@ -210,7 +218,7 @@ def tile_picked_toklapwsum_none_po_kernel(
         out_rows = out_0.rearrange("(p t) j -> p t j", t=PACK)
         out_words = out_1[0].rearrange("p n t -> p (n t)").bitcast(I32)
         out_plane = sb("out_plane", [P, H], U8)
-        out_codes = sb("out_codes", [P, H], U32)
+        out_codes = {}
         result = sb("result", [P, PACK, H], F32)
         out_grouped = sb("out_grouped", [P, H, PACK], BF16)
         third = [sb("third%d" % t, [P, H], F32) for t in range(PACK)]
@@ -239,34 +247,25 @@ def tile_picked_toklapwsum_none_po_kernel(
         def rnd(t0, t1, lo, hi, copy=nc.vector.tensor_copy):
             copy(words_by_four(out_grouped[:, lo:hi, t0:t1]), rows_by_four(result[:, t0:t1, lo:hi]))
 
-        def quant(lo, hi):
-            nc.vector.quantize_mx(out_codes[:, lo:hi].bitcast(FP8X4), out_plane[:, lo:hi], out_grouped[:, lo:hi, :].rearrange("p c t -> p (c t)"))
+        def quant(lo, hi, tag=None):
+            out_codes[lo] = sb("out_codes%d" % lo, [P, hi - lo], U32, tag)
+            nc.vector.quantize_mx(out_codes[lo][:].bitcast(FP8X4), out_plane[:, lo:hi], out_grouped[:, lo:hi, :].rearrange("p c t -> p (c t)"))
 
         def store_words(lo, hi):
-            nc.sync.dma_start(out_words[:, lo:hi], out_codes[:, lo:hi].bitcast(I32))
+            nc.sync.dma_start(out_words[:, lo:hi], out_codes[lo][:].bitcast(I32))
 
         for t in range(4):
             g5(t, 0, 256); p4(t, 0, 256)
             if t > 0:
                 add(t - 1, 0, 256)
             g3(t, 0, 256); p3(t, 0, 256)
-        for t in range(4):
-            g5(t, 256, H); p4(t, 256, H)
-            if t == 0:
-                add(3, 0, 256); store(0, 4, 0, 256)
-            else:
-                add(t - 1, 256, H)
-            gate_h(1, t)
-            if t < 3:
-                g3(t, 256, H); p3(t, 256, H)
-            if t == 0:
-                rnd(0, 4, 0, 256)
-            if t == 1:
-                quant(0, 256); store_words(0, 256)
-            if t == 2:
-                store(0, 2, 256, H); rnd(0, 2, 256, H)
-        g3(3, 256, 384); p3(3, 256, 384)
-        g3(3, 384, H); p3(3, 384, H); add(3, 256, 384); add(3, 384, H); store(2, 4, 256, H); rnd(2, 4, 256, 384); rnd(2, 4, 384, H); quant(256, 384); quant(384, H); store_words(256, H)
+        g5(0, 256, H); p4(0, 256, H); add(3, 0, 256); store(0, 4, 0, 256); gate_h(1, 0); g3(0, 256, H); p3(0, 256, H); rnd(0, 4, 0, 256)
+        g5(1, 256, H); p4(1, 256, H); add(0, 256, H); gate_h(1, 1); g3(1, 256, H); p3(1, 256, H); quant(0, 256); store_words(0, 256)
+        g5(2, 256, H); p4(2, 256, H); add(1, 256, H); store(0, 2, 256, H)
+        g5(3, 256, H); p4(3, 256, H)
+        gate_h(1, 2); g3(2, 256, H); p3(2, 256, H)
+        gate_h(1, 3); g3(3, 256, 384); p3(3, 256, 384); add(2, 256, H); store(2, 3, 256, H)
+        g3(3, 384, H); p3(3, 384, H); rnd(0, 2, 256, H, nc.scalar.copy); add(3, 256, 384); add(3, 384, H); store(3, 4, 256, H); rnd(2, 4, 256, 384); rnd(2, 4, 384, H); quant(256, 384); store_words(256, 384); quant(384, H); store_words(384, H)
 
         for q in range(4):
             queue = nc.sync if q % 2 == 0 else nc.scalar

@@ -14,20 +14,22 @@ MULT = mybir.AluOpType.mult
 COPY = mybir.ActivationFunctionType.Copy
 SIGMOID = mybir.ActivationFunctionType.Sigmoid
 
-FLOPS = 2 * 512 * 512 * 512 * 2
+FLOPS = 2 * (2 * 512 * 512 * 512)
 
 P = 128
 PACK = 4
-T = 2048
-S = 512
+QUADRANTS = 4
+TOKENS = 2048
+ROWS = 512
 H = 512
-BANK = 512
-PER_COL = 16
-
-HALVES = [(0, 256), (256, 512)]
-LAST_PIECES = [(0, 256), (256, 384), (384, 512)]
-WINDOW = 1024
+HALF = H // 2
+QUARTER = H // 4
+HALVES = [(0, HALF), (HALF, H)]
+PER_COLUMN = 16
+LINE = 16
+MIX = 0.75
 WA_SCALAR_COLS = 96
+OWN_ON_VECTOR = 2
 
 
 def tile_picked_toklapwsum_none_po_kernel(
@@ -38,20 +40,23 @@ def tile_picked_toklapwsum_none_po_kernel(
         keep = ctx.enter_context(tc.tile_pool(name="keep", bufs=1))
         psum = ctx.enter_context(tc.psum_pool(name="psum", bufs=1))
 
-        def sb(name, shape, dtype, tag=None):
-            return keep.tile(shape, dtype, name=name, tag=tag or name, align_bytes=64)
+        def sb(name, shape, dtype, buffer=None):
+            return keep.tile(shape, dtype, name=name, tag=buffer or name, align_bytes=64)
 
         def load_list(name, dram):
-            tile = sb(name, [P, S // PER_COL], U16)
+            tile = sb(name, [P, ROWS // PER_COLUMN], U16)
             nc.sync.dma_start(tile[:], dram)
             return tile
 
-        def load_scale_rows(queue, tile, dram):
-            for q in range(4):
-                queue.dma_start(tile[32 * q : 32 * q + 4, :].bitcast(I32), dram[0, 4 * q : 4 * q + 4, :].bitcast(I32))
+        def load_scale_rows(tile, dram):
+            for q in range(QUADRANTS):
+                nc.sync.dma_start(tile[32 * q : 32 * q + 4, :].bitcast(I32), dram[0, 4 * q : 4 * q + 4, :].bitcast(I32))
+
+        def as_words(dram):
+            return dram[0].rearrange("p n t -> p (n t)").bitcast(I32)
 
         def entries(tile, lo, hi):
-            return tile[:, lo // PER_COL : hi // PER_COL]
+            return tile[:, lo // PER_COLUMN : hi // PER_COLUMN]
 
         def deal(dst, src, run):
             nc.vector.tensor_copy(
@@ -59,130 +64,125 @@ def tile_picked_toklapwsum_none_po_kernel(
                 src.rearrange("k (c i t) -> k c t i", i=run, t=PACK),
             )
 
-        def rows_by_four(planes):
-            return planes.rearrange("p t (c i) -> p c t i", i=4)
+        def rows_by_four(row_sets):
+            return row_sets.rearrange("p t (c i) -> p c t i", i=4)
 
         def words_by_four(grouped):
             return grouped.rearrange("p (c i) t -> p c t i", i=4)
 
-        def banks_for(name, lo, hi):
-            width = hi - lo
-            per_bank = BANK // width
-            banks = [psum.tile([P, per_bank, width], F32, name="%s_%d_%d" % (name, lo, b)) for b in range(PACK // per_bank)]
-            return [banks[t // per_bank][:, t % per_bank, :] for t in range(PACK)]
+        def product(name, n, t, codes, code_scales, moving, moving_scales):
+            lo, hi = HALVES[n]
+            acc = psum.tile([P, HALF], F32, name="%s%d_%d" % (name, n, t), tag="bank%d" % (PACK * n + t))
+            nc.tensor.matmul_mx(
+                acc[:], codes[:, t, :].bitcast(FP8X4), code_scales[:, t, :],
+                moving[:, lo:hi].bitcast(FP8X4), moving_scales[:, lo:hi], start=True, stop=True,
+            )
+            return acc
 
+        x_scale_table = sb("x_scale_table", [P, TOKENS], U8)
+        nc.vector.memset(x_scale_table[:].bitcast(I32), 0)
+        w1_scale_table = sb("w1_scale_table", [P, ROWS], U8)
+        nc.vector.memset(w1_scale_table[:].bitcast(I32), 0)
         warm = sb("warm", [P, 8], F32)
-        nc.gpsimd.memset(warm[:, 0:1], 0.0)
+        nc.vector.memset(warm[:, 0:1], 0.0)
         nc.scalar.activation(warm[:, 4:5], warm[:, 0:1], SIGMOID)
-        x_plane = sb("x_plane", [P, T], U8)
-        nc.vector.memset(x_plane[:].bitcast(I32), 0)
-        w1_plane = sb("w1_plane", [P, S], U8)
-        nc.vector.memset(w1_plane[:].bitcast(I32), 0)
 
         wa_rows = wa.rearrange("(p t) j -> p t j", t=PACK)
-        wa_raw = [sb("wa_raw%d" % lo, [P, PACK, hi - lo], F32) for lo, hi in HALVES]
+        wa_raw = [sb("wa_raw%d" % n, [P, PACK, HALF], F32) for n in range(2)]
+        nc.sync.dma_start(wa_raw[0][:], wa_rows[:, :, :HALF])
         offs_t = load_list("offs_t", offs)
-        nc.sync.dma_start(wa_raw[0][:], wa_rows[:, :, slice(*HALVES[0])])
-        load_scale_rows(nc.sync, x_plane, x_scales)
-        x_table = sb("x_table", [P, T], U32)
-        nc.sync.dma_start(x_table[:].bitcast(I32), x_words[0].rearrange("p n t -> p (n t)").bitcast(I32))
-        nc.sync.dma_start(wa_raw[1][:], wa_rows[:, :, slice(*HALVES[1])])
+        load_scale_rows(x_scale_table, x_scales)
+        x_table = sb("x_table", [P, TOKENS], U32)
+        nc.sync.dma_start(x_table[:].bitcast(I32), as_words(x_words))
+        nc.sync.dma_start(wa_raw[1][:], wa_rows[:, :, HALF:])
         gt_t = sb("gt_t", [P, PACK], F32)
         nc.sync.dma_start(gt_t[:], gt.rearrange("(p t) o -> p (t o)", t=PACK))
-        load_scale_rows(nc.sync, w1_plane, w1_scales)
-        w1_table = sb("w1_table", [P, S], I32)
-        nc.sync.dma_start(w1_table[:], w1_words[0].rearrange("p n t -> p (n t)").bitcast(I32))
+        load_scale_rows(w1_scale_table, w1_scales)
+        w1_table = sb("w1_table", [P, ROWS], I32)
+        nc.sync.dma_start(w1_table[:], as_words(w1_words))
         n2_t = load_list("n2_t", n2)
         n1_t = load_list("n1_t", n1)
         n5_t = load_list("n5_t", n5)
         n4_t = load_list("n4_t", n4)
         n3_t = load_list("n3_t", n3)
 
-        wa_codes = sb("wa_codes", [P, H], U32)
-        wa_plane = sb("wa_plane", [P, H], U8)
+        wa_codes = sb("wa_codes", [P, H], U32, "x_scale_table")
+        wa_scales = sb("wa_scales", [P, H], U8)
 
-        def quantise_wa(n, cut):
+        def quantise_wa(n, scalar_cols):
             lo, hi = HALVES[n]
-            grouped = sb("wa_grouped%d" % lo, [P, hi - lo, PACK], BF16, "staging%d" % n)
-            nc.scalar.copy(words_by_four(grouped[:, :cut, :]), rows_by_four(wa_raw[n][:, :, :cut]))
-            if cut < hi - lo:
-                nc.vector.tensor_copy(words_by_four(grouped[:, cut:, :]), rows_by_four(wa_raw[n][:, :, cut:]))
-            nc.vector.quantize_mx(wa_codes[:, lo:hi].bitcast(FP8X4), wa_plane[:, lo:hi], grouped[:].rearrange("p c t -> p (c t)"))
+            grouped = sb("wa_grouped%d" % n, [P, HALF, PACK], BF16)
+            nc.scalar.copy(words_by_four(grouped[:, :scalar_cols, :]), rows_by_four(wa_raw[n][:, :, :scalar_cols]))
+            if scalar_cols < HALF:
+                nc.vector.tensor_copy(words_by_four(grouped[:, scalar_cols:, :]), rows_by_four(wa_raw[n][:, :, scalar_cols:]))
+            nc.vector.quantize_mx(wa_codes[:, lo:hi].bitcast(FP8X4), wa_scales[:, lo:hi], grouped[:].rearrange("p c t -> p (c t)"))
 
-        x_bytes = sb("x_bytes", [P, S], U8)
-        nc.vector.tensor_copy(x_bytes[:], x_plane[:].indirect(offs_t[:]))
-        x_dealt_bytes = sb("x_dealt_bytes", [P, PACK, P], U8)
-        deal(x_dealt_bytes[:], x_bytes[:], 16)
-        quantise_wa(0, 256)
-        x_codes = sb("x_codes", [P, PACK, P], U32)
-        nc.vector.tensor_copy(x_codes[:].rearrange("k t m -> k m t"), x_table[:].indirect(offs_t[:]))
+        picked_scales = sb("picked_scales", [P, ROWS], U8)
+        nc.vector.tensor_copy(picked_scales[:], x_scale_table[:].indirect(offs_t[:]))
+        x_dealt_scales = sb("x_dealt_scales", [P, PACK, P], U8)
+        deal(x_dealt_scales[:], picked_scales[:], LINE)
+        quantise_wa(0, HALF)
+        x_dealt_codes = sb("x_dealt_codes", [P, PACK, P], U32, "picked_scales")
+        nc.vector.tensor_copy(x_dealt_codes[:].rearrange("k t m -> k m t"), x_table[:].indirect(offs_t[:]))
         quantise_wa(1, WA_SCALAR_COLS)
-        gt_mix = sb("gt_mix", [P, PACK], F32)
-        nc.vector.tensor_scalar(gt_mix[:], gt_t[:], 0.75, None, MULT)
-        gt_neg = sb("gt_neg", [P, PACK], F32)
-        nc.vector.tensor_scalar(gt_neg[:], gt_t[:], -1.0, None, MULT)
+        weights = sb("weights", [P, 2, PACK], F32, "wa_raw1")
+        mix_weight = weights[:, 0, :]
+        nc.scalar.activation(mix_weight, gt_t[:], COPY, scale=MIX)
+        own_weight = weights[:, 1, :]
+        nc.scalar.activation(own_weight, gt_t[:], COPY, scale=-1.0)
 
         y_win = [sb("y_win%d" % t, [P, H], F32) for t in range(PACK)]
         own = [sb("own%d" % t, [P, H], F32) for t in range(PACK)]
-
-        def product(name, n, t, codes, planes, moving, moving_plane):
-            lo, hi = HALVES[n]
-            acc = psum.tile([P, hi - lo], F32, name="%s%d_%d" % (name, n, t), tag="bank%d" % (PACK * n + t))
-            nc.tensor.matmul_mx(
-                acc[:], codes[:, t, :].bitcast(FP8X4), planes[:, t, :],
-                moving[:, lo:hi].bitcast(FP8X4), moving_plane[:, lo:hi], start=True, stop=True,
-            )
-            return acc
-
-        def own_term(n, t):
-            lo, hi = HALVES[n]
-            nc.vector.tensor_scalar(own[t][:, lo:hi], y_win[t][:, lo:hi], -4.0 / 3.0, None, MULT)
-
-        def own_from_bank(n, t):
-            lo, hi = HALVES[n]
-            nc.scalar.activation(own[t][:, lo:hi], y_acc[n, t][:], COPY, scale=gt_neg[:, t : t + 1])
-
         y_acc = {}
         for n, (lo, hi) in enumerate(HALVES):
             for t in range(PACK):
-                y_acc[n, t] = product("y_acc", n, t, x_codes, x_dealt_bytes, wa_codes, wa_plane)
-                nc.scalar.activation(y_win[t][:, lo:hi], y_acc[n, t][:], COPY, scale=gt_mix[:, t : t + 1])
+                y_acc[n, t] = product("y_acc", n, t, x_dealt_codes, x_dealt_scales, wa_codes, wa_scales)
+                nc.scalar.activation(y_win[t][:, lo:hi], y_acc[n, t][:], COPY, scale=mix_weight[:, t : t + 1])
 
-        w1_codes = sb("w1_codes", [P, PACK, P], I32, "staging1")
-        deal(w1_codes[:], w1_table[:], 4)
-        w1_dealt_bytes = sb("w1_dealt_bytes", [P, PACK, P], U8)
-        deal(w1_dealt_bytes[:], w1_plane[:], 16)
+        def own_from_window(n, t):
+            lo, hi = HALVES[n]
+            nc.vector.tensor_scalar(own[t][:, lo:hi], y_win[t][:, lo:hi], -1.0 / MIX, None, MULT)
+
+        def own_from_bank(n, t):
+            lo, hi = HALVES[n]
+            nc.scalar.activation(own[t][:, lo:hi], y_acc[n, t][:], COPY, scale=own_weight[:, t : t + 1])
+
+        w1_dealt_codes = sb("w1_dealt_codes", [P, PACK, P], I32, "wa_grouped1")
+        deal(w1_dealt_codes[:], w1_table[:], LINE // 4)
+        w1_dealt_scales = sb("w1_dealt_scales", [P, PACK, P], U8)
+        deal(w1_dealt_scales[:], w1_scale_table[:], LINE)
         for t in range(PACK):
-            own_term(0, t)
+            own_from_window(0, t)
 
         z_codes = sb("z_codes", [P, H], U32)
-        z_plane = sb("z_plane", [P, H], U8)
+        z_scales = sb("z_scales", [P, H], U8)
         h_win = [sb("h_win%d" % t, [P, H], F32) for t in range(PACK)]
-        h_gate = [sb("h_gate%d" % t, [P, H], F32) for t in range(PACK)]
-        first = [sb("first%d" % lo, [P, PACK, hi - lo], F32) for lo, hi in HALVES]
-        second = {}
+        y_at_n1 = [sb("y_at_n1_%d" % n, [P, PACK, HALF], F32) for n in range(2)]
+        y_at_n2 = [sb("y_at_n2_%d" % n, [P, PACK, HALF], F32) for n in range(2)]
         z_grouped = {}
         h_acc = {}
+        half_tiles = {}
 
-        def first_term(n, t):
-            lo, hi = HALVES[n]
-            nc.scalar.activation(first[n][:, t, :], y_win[t][:].indirect(entries(n1_t, lo, hi)), COPY)
+        def half_of(name, t, lo, hi):
+            n = lo // HALF
+            if (name, t, n) not in half_tiles:
+                half_tiles[name, t, n] = sb("%s%d_%d" % (name, t, n), [P, HALF], F32, "%s%d" % (name, t))
+            return half_tiles[name, t, n][:, lo - HALF * n : hi - HALF * n]
 
-        def second_term(n, t):
+        def look_up_y(n, t):
             lo, hi = HALVES[n]
-            if t == 0:
-                second[n] = sb("second%d" % lo, [P, PACK, hi - lo], F32, None)
-            nc.vector.tensor_tensor(second[n][:, t, :], y_win[t][:].indirect(entries(n2_t, lo, hi)), own[t][:, lo:hi], ADD)
+            nc.scalar.activation(y_at_n1[n][:, t, :], y_win[t][:].indirect(entries(n1_t, lo, hi)), COPY)
+            nc.vector.tensor_tensor(y_at_n2[n][:, t, :], y_win[t][:].indirect(entries(n2_t, lo, hi)), own[t][:, lo:hi], ADD)
 
         def sum_z(n):
-            z_grouped[n] = sb("z_grouped%d" % n, [P, H // 2, PACK], BF16, "z_grouped")
-            nc.vector.tensor_tensor(words_by_four(z_grouped[n][:]), rows_by_four(first[n][:]), rows_by_four(second[n][:]), ADD)
+            z_grouped[n] = sb("z_grouped%d" % n, [P, HALF, PACK], BF16, "z_grouped")
+            nc.vector.tensor_tensor(words_by_four(z_grouped[n][:]), rows_by_four(y_at_n1[n][:]), rows_by_four(y_at_n2[n][:]), ADD)
 
         def multiply_z(n):
             lo, hi = HALVES[n]
-            nc.vector.quantize_mx(z_codes[:, lo:hi].bitcast(FP8X4), z_plane[:, lo:hi], z_grouped[n][:].rearrange("p c t -> p (c t)"))
+            nc.vector.quantize_mx(z_codes[:, lo:hi].bitcast(FP8X4), z_scales[:, lo:hi], z_grouped[n][:].rearrange("p c t -> p (c t)"))
             for t in range(PACK):
-                h_acc[n, t] = product("h_acc", n, t, w1_codes, w1_dealt_bytes, z_codes, z_plane)
+                h_acc[n, t] = product("h_acc", n, t, w1_dealt_codes, w1_dealt_scales, z_codes, z_scales)
 
         def fetch_h(n, t, copy):
             lo, hi = HALVES[n]
@@ -190,20 +190,18 @@ def tile_picked_toklapwsum_none_po_kernel(
 
         def gate_h(n, t):
             lo, hi = HALVES[n]
-            nc.scalar.activation(h_gate[t][:, lo:hi], h_acc[n, t][:], SIGMOID)
+            nc.scalar.activation(half_of("h_gate", t, lo, hi), h_acc[n, t][:], SIGMOID)
 
         for t in range(PACK):
-            first_term(0, t)
-            second_term(0, t)
+            look_up_y(0, t)
         for t in range(PACK):
-            if t < 2:
-                own_term(1, t)
+            if t < OWN_ON_VECTOR:
+                own_from_window(1, t)
             else:
                 own_from_bank(1, t)
         sum_z(0)
         for t in range(PACK):
-            first_term(1, t)
-            second_term(1, t)
+            look_up_y(1, t)
             if t == 0:
                 multiply_z(0)
         for t in range(PACK):
@@ -216,57 +214,76 @@ def tile_picked_toklapwsum_none_po_kernel(
             fetch_h(1, t, nc.vector.tensor_copy)
 
         out_rows = out_0.rearrange("(p t) j -> p t j", t=PACK)
-        out_words = out_1[0].rearrange("p n t -> p (n t)").bitcast(I32)
-        out_plane = sb("out_plane", [P, H], U8)
-        out_codes = {}
+        out_words = as_words(out_1)
+        out_scales = sb("out_scales", [P, H], U8)
         result = sb("result", [P, PACK, H], F32)
         out_grouped = sb("out_grouped", [P, H, PACK], BF16)
-        third = [sb("third%d" % t, [P, H], F32) for t in range(PACK)]
-        fifth = [sb("fifth%d" % t, [P, H], F32) for t in range(PACK)]
         left = [sb("left%d" % t, [P, H], F32) for t in range(PACK)]
         right = [sb("right%d" % t, [P, H], F32) for t in range(PACK)]
 
-        def g5(t, lo, hi):
-            nc.scalar.activation(fifth[t][:, lo:hi], h_win[t][:].indirect(entries(n5_t, lo, hi)), SIGMOID)
+        def right_term(t, lo, hi):
+            nc.scalar.activation(half_of("gate_at_n5", t, lo, hi), h_win[t][:].indirect(entries(n5_t, lo, hi)), SIGMOID)
+            nc.vector.tensor_tensor(right[t][:, lo:hi], h_win[t][:].indirect(entries(n4_t, lo, hi)), half_of("gate_at_n5", t, lo, hi), MULT)
 
-        def p4(t, lo, hi):
-            nc.vector.tensor_tensor(right[t][:, lo:hi], h_win[t][:].indirect(entries(n4_t, lo, hi)), fifth[t][:, lo:hi], MULT)
+        def left_term(t, lo, hi):
+            nc.scalar.activation(half_of("h_at_n3", t, lo, hi), h_win[t][:].indirect(entries(n3_t, lo, hi)), COPY)
+            nc.vector.tensor_tensor(left[t][:, lo:hi], half_of("h_at_n3", t, lo, hi), half_of("h_gate", t, lo, hi), MULT)
 
-        def g3(t, lo, hi):
-            nc.scalar.activation(third[t][:, lo:hi], h_win[t][:].indirect(entries(n3_t, lo, hi)), COPY)
-
-        def p3(t, lo, hi):
-            nc.vector.tensor_tensor(left[t][:, lo:hi], third[t][:, lo:hi], h_gate[t][:, lo:hi], MULT)
-
-        def add(t, lo, hi):
+        def add_terms(t, lo, hi):
             nc.vector.tensor_tensor(result[:, t, lo:hi], left[t][:, lo:hi], right[t][:, lo:hi], ADD)
 
-        def store(t0, t1, lo, hi):
-            nc.sync.dma_start(out_rows[:, t0:t1, lo:hi], result[:, t0:t1, lo:hi])
+        def store_rows(t_lo, t_hi, lo, hi):
+            nc.sync.dma_start(out_rows[:, t_lo:t_hi, lo:hi], result[:, t_lo:t_hi, lo:hi])
 
-        def rnd(t0, t1, lo, hi, copy=nc.vector.tensor_copy):
-            copy(words_by_four(out_grouped[:, lo:hi, t0:t1]), rows_by_four(result[:, t0:t1, lo:hi]))
+        def round_rows(t_lo, t_hi, lo, hi, copy):
+            copy(words_by_four(out_grouped[:, lo:hi, t_lo:t_hi]), rows_by_four(result[:, t_lo:t_hi, lo:hi]))
 
-        def quant(lo, hi, tag=None):
-            out_codes[lo] = sb("out_codes%d" % lo, [P, hi - lo], U32, tag)
-            nc.vector.quantize_mx(out_codes[lo][:].bitcast(FP8X4), out_plane[:, lo:hi], out_grouped[:, lo:hi, :].rearrange("p c t -> p (c t)"))
+        def quantise_out(lo, hi):
+            codes = sb("out_codes%d" % lo, [P, hi - lo], U32)
+            nc.vector.quantize_mx(codes[:].bitcast(FP8X4), out_scales[:, lo:hi], out_grouped[:, lo:hi, :].rearrange("p c t -> p (c t)"))
+            nc.sync.dma_start(out_words[:, lo:hi], codes[:].bitcast(I32))
 
-        def store_words(lo, hi):
-            nc.sync.dma_start(out_words[:, lo:hi], out_codes[lo][:].bitcast(I32))
-
-        for t in range(4):
-            g5(t, 0, 256); p4(t, 0, 256)
+        for t in range(PACK):
+            right_term(t, 0, HALF)
             if t > 0:
-                add(t - 1, 0, 256)
-            g3(t, 0, 256); p3(t, 0, 256)
-        g5(0, 256, H); p4(0, 256, H); add(3, 0, 256); store(0, 4, 0, 256); gate_h(1, 0); g3(0, 256, H); p3(0, 256, H); rnd(0, 4, 0, 256)
-        g5(1, 256, H); p4(1, 256, H); add(0, 256, H); gate_h(1, 1); g3(1, 256, H); p3(1, 256, H); quant(0, 256); store_words(0, 256)
-        g5(2, 256, H); p4(2, 256, H); add(1, 256, H); store(0, 2, 256, H)
-        g5(3, 256, H); p4(3, 256, H)
-        gate_h(1, 2); g3(2, 256, H); p3(2, 256, H)
-        gate_h(1, 3); g3(3, 256, 384); p3(3, 256, 384); add(2, 256, H); store(2, 3, 256, H)
-        g3(3, 384, H); p3(3, 384, H); rnd(0, 2, 256, H, nc.scalar.copy); add(3, 256, 384); add(3, 384, H); store(3, 4, 256, H); rnd(2, 4, 256, 384); rnd(2, 4, 384, H); quant(256, 384); store_words(256, 384); quant(384, H); store_words(384, H)
+                add_terms(t - 1, 0, HALF)
+            left_term(t, 0, HALF)
 
-        for q in range(4):
+        right_term(0, HALF, H)
+        add_terms(3, 0, HALF)
+        store_rows(0, PACK, 0, HALF)
+        gate_h(1, 0)
+        left_term(0, HALF, H)
+        round_rows(0, PACK, 0, HALF, nc.vector.tensor_copy)
+
+        right_term(1, HALF, H)
+        add_terms(0, HALF, H)
+        gate_h(1, 1)
+        left_term(1, HALF, H)
+        quantise_out(0, HALF)
+
+        right_term(2, HALF, H)
+        add_terms(1, HALF, H)
+        store_rows(0, 2, HALF, H)
+
+        right_term(3, HALF, H)
+        gate_h(1, 2)
+        left_term(2, HALF, H)
+        gate_h(1, 3)
+        quarters = [(HALF, HALF + QUARTER), (HALF + QUARTER, H)]
+        left_term(3, *quarters[0])
+        add_terms(2, HALF, H)
+        store_rows(2, 3, HALF, H)
+        left_term(3, *quarters[1])
+        round_rows(0, 2, HALF, H, nc.scalar.copy)
+        for lo, hi in quarters:
+            add_terms(3, lo, hi)
+        store_rows(3, PACK, HALF, H)
+        for lo, hi in quarters:
+            round_rows(2, PACK, lo, hi, nc.vector.tensor_copy)
+        for lo, hi in quarters:
+            quantise_out(lo, hi)
+
+        for q in range(QUADRANTS):
             queue = nc.sync if q % 2 == 0 else nc.scalar
-            queue.dma_start(out_2[0, 4 * q : 4 * q + 4, :].bitcast(I32), out_plane[32 * q : 32 * q + 4, :].bitcast(I32))
+            queue.dma_start(out_2[0, 4 * q : 4 * q + 4, :].bitcast(I32), out_scales[32 * q : 32 * q + 4, :].bitcast(I32))

from contextlib import ExitStack

import concourse.mybir as mybir

F32 = mybir.dt.float32
BF16 = mybir.dt.bfloat16
I32 = mybir.dt.int32
U32 = mybir.dt.uint32
U16 = mybir.dt.uint16
U8 = mybir.dt.uint8
FP8X4 = mybir.dt.float8_e4m3fn_x4
ADD = mybir.AluOpType.add
MULT = mybir.AluOpType.mult
COPY = mybir.ActivationFunctionType.Copy
SIGMOID = mybir.ActivationFunctionType.Sigmoid

FLOPS = 2 * (2 * 512 * 512 * 512)

P = 128
PACK = 4
QUADRANTS = 4
TOKENS = 2048
ROWS = 512
H = 512
HALF = H // 2
QUARTER = H // 4
HALVES = [(0, HALF), (HALF, H)]
PER_COLUMN = 16
LINE = 16
MIX = 0.75
WA_SCALAR_COLS = 96
OWN_ON_VECTOR = 2


def tile_picked_toklapwsum_none_po_kernel(
    tc, x_words, x_scales, wa, gt, w1_words, w1_scales, offs, n1, n2, n3, n4, n5, out_0, out_1, out_2
):
    nc = tc.nc
    with ExitStack() as ctx:
        keep = ctx.enter_context(tc.tile_pool(name="keep", bufs=1))
        psum = ctx.enter_context(tc.psum_pool(name="psum", bufs=1))

        def sb(name, shape, dtype, buffer=None):
            return keep.tile(shape, dtype, name=name, tag=buffer or name, align_bytes=64)

        def load_list(name, dram):
            tile = sb(name, [P, ROWS // PER_COLUMN], U16)
            nc.sync.dma_start(tile[:], dram)
            return tile

        def load_scale_rows(tile, dram):
            for q in range(QUADRANTS):
                nc.sync.dma_start(tile[32 * q : 32 * q + 4, :].bitcast(I32), dram[0, 4 * q : 4 * q + 4, :].bitcast(I32))

        def as_words(dram):
            return dram[0].rearrange("p n t -> p (n t)").bitcast(I32)

        def entries(tile, lo, hi):
            return tile[:, lo // PER_COLUMN : hi // PER_COLUMN]

        def deal(dst, src, run):
            nc.vector.tensor_copy(
                dst.rearrange("k t (c i) -> k c t i", i=run),
                src.rearrange("k (c i t) -> k c t i", i=run, t=PACK),
            )

        def rows_by_four(row_sets):
            return row_sets.rearrange("p t (c i) -> p c t i", i=4)

        def words_by_four(grouped):
            return grouped.rearrange("p (c i) t -> p c t i", i=4)

        def product(name, n, t, codes, code_scales, moving, moving_scales):
            lo, hi = HALVES[n]
            acc = psum.tile([P, HALF], F32, name="%s%d_%d" % (name, n, t), tag="bank%d" % (PACK * n + t))
            nc.tensor.matmul_mx(
                acc[:], codes[:, t, :].bitcast(FP8X4), code_scales[:, t, :],
                moving[:, lo:hi].bitcast(FP8X4), moving_scales[:, lo:hi], start=True, stop=True,
            )
            return acc

        x_scale_table = sb("x_scale_table", [P, TOKENS], U8)
        nc.vector.memset(x_scale_table[:].bitcast(I32), 0)
        w1_scale_table = sb("w1_scale_table", [P, ROWS], U8)
        nc.vector.memset(w1_scale_table[:].bitcast(I32), 0)
        warm = sb("warm", [P, 8], F32)
        nc.vector.memset(warm[:, 0:1], 0.0)
        nc.scalar.activation(warm[:, 4:5], warm[:, 0:1], SIGMOID)

        wa_rows = wa.rearrange("(p t) j -> p t j", t=PACK)
        wa_raw = [sb("wa_raw%d" % n, [P, PACK, HALF], F32) for n in range(2)]
        nc.sync.dma_start(wa_raw[0][:], wa_rows[:, :, :HALF])
        offs_t = load_list("offs_t", offs)
        load_scale_rows(x_scale_table, x_scales)
        x_table = sb("x_table", [P, TOKENS], U32)
        nc.sync.dma_start(x_table[:].bitcast(I32), as_words(x_words))
        nc.sync.dma_start(wa_raw[1][:], wa_rows[:, :, HALF:])
        gt_t = sb("gt_t", [P, PACK], F32)
        nc.sync.dma_start(gt_t[:], gt.rearrange("(p t) o -> p (t o)", t=PACK))
        load_scale_rows(w1_scale_table, w1_scales)
        w1_table = sb("w1_table", [P, ROWS], I32)
        nc.sync.dma_start(w1_table[:], as_words(w1_words))
        n2_t = load_list("n2_t", n2)
        n1_t = load_list("n1_t", n1)
        n5_t = load_list("n5_t", n5)
        n4_t = load_list("n4_t", n4)
        n3_t = load_list("n3_t", n3)

        wa_codes = sb("wa_codes", [P, H], U32, "x_scale_table")
        wa_scales = sb("wa_scales", [P, H], U8)

        def quantise_wa(n, scalar_cols):
            lo, hi = HALVES[n]
            grouped = sb("wa_grouped%d" % n, [P, HALF, PACK], BF16)
            nc.scalar.copy(words_by_four(grouped[:, :scalar_cols, :]), rows_by_four(wa_raw[n][:, :, :scalar_cols]))
            if scalar_cols < HALF:
                nc.vector.tensor_copy(words_by_four(grouped[:, scalar_cols:, :]), rows_by_four(wa_raw[n][:, :, scalar_cols:]))
            nc.vector.quantize_mx(wa_codes[:, lo:hi].bitcast(FP8X4), wa_scales[:, lo:hi], grouped[:].rearrange("p c t -> p (c t)"))

        picked_scales = sb("picked_scales", [P, ROWS], U8)
        nc.vector.tensor_copy(picked_scales[:], x_scale_table[:].indirect(offs_t[:]))
        x_dealt_scales = sb("x_dealt_scales", [P, PACK, P], U8)
        deal(x_dealt_scales[:], picked_scales[:], LINE)
        quantise_wa(0, HALF)
        x_dealt_codes = sb("x_dealt_codes", [P, PACK, P], U32, "picked_scales")
        nc.vector.tensor_copy(x_dealt_codes[:].rearrange("k t m -> k m t"), x_table[:].indirect(offs_t[:]))
        quantise_wa(1, WA_SCALAR_COLS)
        weights = sb("weights", [P, 2, PACK], F32, "wa_raw1")
        mix_weight = weights[:, 0, :]
        nc.scalar.activation(mix_weight, gt_t[:], COPY, scale=MIX)
        own_weight = weights[:, 1, :]
        nc.scalar.activation(own_weight, gt_t[:], COPY, scale=-1.0)

        y_win = [sb("y_win%d" % t, [P, H], F32) for t in range(PACK)]
        own = [sb("own%d" % t, [P, H], F32) for t in range(PACK)]
        y_acc = {}
        for n, (lo, hi) in enumerate(HALVES):
            for t in range(PACK):
                y_acc[n, t] = product("y_acc", n, t, x_dealt_codes, x_dealt_scales, wa_codes, wa_scales)
                nc.scalar.activation(y_win[t][:, lo:hi], y_acc[n, t][:], COPY, scale=mix_weight[:, t : t + 1])

        def own_from_window(n, t):
            lo, hi = HALVES[n]
            nc.vector.tensor_scalar(own[t][:, lo:hi], y_win[t][:, lo:hi], -1.0 / MIX, None, MULT)

        def own_from_bank(n, t):
            lo, hi = HALVES[n]
            nc.scalar.activation(own[t][:, lo:hi], y_acc[n, t][:], COPY, scale=own_weight[:, t : t + 1])

        w1_dealt_codes = sb("w1_dealt_codes", [P, PACK, P], I32, "wa_grouped1")
        deal(w1_dealt_codes[:], w1_table[:], LINE // 4)
        w1_dealt_scales = sb("w1_dealt_scales", [P, PACK, P], U8)
        deal(w1_dealt_scales[:], w1_scale_table[:], LINE)
        for t in range(PACK):
            own_from_window(0, t)

        z_codes = sb("z_codes", [P, H], U32)
        z_scales = sb("z_scales", [P, H], U8)
        h_win = [sb("h_win%d" % t, [P, H], F32) for t in range(PACK)]
        y_at_n1 = [sb("y_at_n1_%d" % n, [P, PACK, HALF], F32) for n in range(2)]
        y_at_n2 = [sb("y_at_n2_%d" % n, [P, PACK, HALF], F32) for n in range(2)]
        z_grouped = {}
        h_acc = {}
        half_tiles = {}

        def half_of(name, t, lo, hi):
            n = lo // HALF
            if (name, t, n) not in half_tiles:
                half_tiles[name, t, n] = sb("%s%d_%d" % (name, t, n), [P, HALF], F32, "%s%d" % (name, t))
            return half_tiles[name, t, n][:, lo - HALF * n : hi - HALF * n]

        def look_up_y(n, t):
            lo, hi = HALVES[n]
            nc.scalar.activation(y_at_n1[n][:, t, :], y_win[t][:].indirect(entries(n1_t, lo, hi)), COPY)
            nc.vector.tensor_tensor(y_at_n2[n][:, t, :], y_win[t][:].indirect(entries(n2_t, lo, hi)), own[t][:, lo:hi], ADD)

        def sum_z(n):
            z_grouped[n] = sb("z_grouped%d" % n, [P, HALF, PACK], BF16, "z_grouped")
            nc.vector.tensor_tensor(words_by_four(z_grouped[n][:]), rows_by_four(y_at_n1[n][:]), rows_by_four(y_at_n2[n][:]), ADD)

        def multiply_z(n):
            lo, hi = HALVES[n]
            nc.vector.quantize_mx(z_codes[:, lo:hi].bitcast(FP8X4), z_scales[:, lo:hi], z_grouped[n][:].rearrange("p c t -> p (c t)"))
            for t in range(PACK):
                h_acc[n, t] = product("h_acc", n, t, w1_dealt_codes, w1_dealt_scales, z_codes, z_scales)

        def fetch_h(n, t, copy):
            lo, hi = HALVES[n]
            copy(h_win[t][:, lo:hi], h_acc[n, t][:])

        def gate_h(n, t):
            lo, hi = HALVES[n]
            nc.scalar.activation(half_of("h_gate", t, lo, hi), h_acc[n, t][:], SIGMOID)

        for t in range(PACK):
            look_up_y(0, t)
        for t in range(PACK):
            if t < OWN_ON_VECTOR:
                own_from_window(1, t)
            else:
                own_from_bank(1, t)
        sum_z(0)
        for t in range(PACK):
            look_up_y(1, t)
            if t == 0:
                multiply_z(0)
        for t in range(PACK):
            fetch_h(0, t, nc.scalar.copy)
        sum_z(1)
        multiply_z(1)
        for t in range(PACK):
            gate_h(0, t)
        for t in range(PACK):
            fetch_h(1, t, nc.vector.tensor_copy)

        out_rows = out_0.rearrange("(p t) j -> p t j", t=PACK)
        out_words = as_words(out_1)
        out_scales = sb("out_scales", [P, H], U8)
        result = sb("result", [P, PACK, H], F32)
        out_grouped = sb("out_grouped", [P, H, PACK], BF16)
        left = [sb("left%d" % t, [P, H], F32) for t in range(PACK)]
        right = [sb("right%d" % t, [P, H], F32) for t in range(PACK)]

        def right_term(t, lo, hi):
            nc.scalar.activation(half_of("gate_at_n5", t, lo, hi), h_win[t][:].indirect(entries(n5_t, lo, hi)), SIGMOID)
            nc.vector.tensor_tensor(right[t][:, lo:hi], h_win[t][:].indirect(entries(n4_t, lo, hi)), half_of("gate_at_n5", t, lo, hi), MULT)

        def left_term(t, lo, hi):
            nc.scalar.activation(half_of("h_at_n3", t, lo, hi), h_win[t][:].indirect(entries(n3_t, lo, hi)), COPY)
            nc.vector.tensor_tensor(left[t][:, lo:hi], half_of("h_at_n3", t, lo, hi), half_of("h_gate", t, lo, hi), MULT)

        def add_terms(t, lo, hi):
            nc.vector.tensor_tensor(result[:, t, lo:hi], left[t][:, lo:hi], right[t][:, lo:hi], ADD)

        def store_rows(t_lo, t_hi, lo, hi):
            nc.sync.dma_start(out_rows[:, t_lo:t_hi, lo:hi], result[:, t_lo:t_hi, lo:hi])

        def round_rows(t_lo, t_hi, lo, hi, copy):
            copy(words_by_four(out_grouped[:, lo:hi, t_lo:t_hi]), rows_by_four(result[:, t_lo:t_hi, lo:hi]))

        def quantise_out(lo, hi):
            codes = sb("out_codes%d" % lo, [P, hi - lo], U32)
            nc.vector.quantize_mx(codes[:].bitcast(FP8X4), out_scales[:, lo:hi], out_grouped[:, lo:hi, :].rearrange("p c t -> p (c t)"))
            nc.sync.dma_start(out_words[:, lo:hi], codes[:].bitcast(I32))

        for t in range(PACK):
            right_term(t, 0, HALF)
            if t > 0:
                add_terms(t - 1, 0, HALF)
            left_term(t, 0, HALF)

        right_term(0, HALF, H)
        add_terms(3, 0, HALF)
        store_rows(0, PACK, 0, HALF)
        gate_h(1, 0)
        left_term(0, HALF, H)
        round_rows(0, PACK, 0, HALF, nc.vector.tensor_copy)

        right_term(1, HALF, H)
        add_terms(0, HALF, H)
        gate_h(1, 1)
        left_term(1, HALF, H)
        quantise_out(0, HALF)

        right_term(2, HALF, H)
        add_terms(1, HALF, H)
        store_rows(0, 2, HALF, H)

        right_term(3, HALF, H)
        gate_h(1, 2)
        left_term(2, HALF, H)
        gate_h(1, 3)
        quarters = [(HALF, HALF + QUARTER), (HALF + QUARTER, H)]
        left_term(3, *quarters[0])
        add_terms(2, HALF, H)
        store_rows(2, 3, HALF, H)
        left_term(3, *quarters[1])
        round_rows(0, 2, HALF, H, nc.scalar.copy)
        for lo, hi in quarters:
            add_terms(3, lo, hi)
        store_rows(3, PACK, HALF, H)
        for lo, hi in quarters:
            round_rows(2, PACK, lo, hi, nc.vector.tensor_copy)
        for lo, hi in quarters:
            quantise_out(lo, hi)

        for q in range(QUADRANTS):
            queue = nc.sync if q % 2 == 0 else nc.scalar
            queue.dma_start(out_2[0, 4 * q : 4 * q + 4, :].bitcast(I32), out_scales[32 * q : 32 * q + 4, :].bitcast(I32))
